import numpy as np, ml_dtypes
CORES = [24,26,29,31,48,50,53,55]
N = 8
import mx_ref
NC = 256
BF = ml_dtypes.bfloat16
def setup_inputs(rng):
    def f(*shape):
        return mx_ref.flush((rng.standard_normal(shape, dtype=np.float32) * np.exp2(rng.integers(-2, 3, shape[:-1] + (1,)))).astype(BF))
    return {"w": f(N, 128, 512), "x": f(N, 128, N * 4 * NC)}
def setup_inputs_blocks(rng):
    d = setup_inputs(rng)
    for k in ("w", "x"): d[k] = mx_ref.spread(d[k], rng, 4)
    return d
def setup_inputs_wide(rng):
    d = setup_inputs(rng)
    for k in ("w", "x"): d[k] = mx_ref.flush((d[k].astype(np.float32) * np.exp2(rng.integers(-8, 9, (N, 1, 1))).astype(np.float32)).astype(BF))
    return d
def setup_inputs_zeros(rng):
    d = setup_inputs(rng); v = d["x"].reshape(N, 128, -1, 4).copy()
    v[np.broadcast_to((rng.random((N, 1, v.shape[2], 1)) < 0.33), v.shape)] = 0
    d["x"] = v.reshape(d["x"].shape)
    return d
def reference(w, x):
    y = np.zeros((N, 128, N * NC), np.float32)
    for r in range(N):
        qw = mx_ref.quantize(w[r])
        for j in range(N):
            y[r][:, NC * j:NC * j + NC] = mx_ref.matmul(qw, mx_ref.quantize(x[j][:, 4 * NC * r:4 * NC * r + 4 * NC]))
    return {"y": y}

from concourse.bass import DstId, RemoteDMATransfer
from concourse.mybir import dt, ActivationFunctionType

N = 8
NC = 256
XC = 4 * NC
SIM_CORES = 64
UNITS = 6

SCRATCH = {
    "xb": ("sbuf", [128, N * XC], "bfloat16"),
    "wb": ("sbuf", [128, 512], "bfloat16"),
    "qx": ("sbuf", [128, N * NC], "float8_e4m3fn_x4"),
    "sx": ("sbuf", [128, N * NC], "uint8"),
    "qw": ("sbuf", [128, 128], "float8_e4m3fn_x4"),
    "sw": ("sbuf", [128, 128], "uint8"),
    "rq": ("sbuf", [128, N * NC], "float8_e4m3fn_x4"),
    "rs": ("sbuf", [128, N * NC], "uint8"),
    "yb": ("sbuf", [128, N * NC], "float32"),
    "ps": ("psum", [128, 512 * UNITS], "float32"),
}
SEMAPHORES = (["ld%d" % i for i in range(5)] + ["qd%d" % i for i in range(N)] + ["qdw"]
              + ["arr%d" % i for i in range(N)] + ["h0", "h1", "h2"]
              + ["mm%d" % i for i in range(UNITS)] + ["cp%d" % i for i in range(UNITS)] + ["stA", "stB", "sent"])


def bits(mask):
    return [e for e in range(mask.bit_length()) if (mask >> e) & 1]


def to_mask(engines):
    m = 0
    for e in engines:
        m |= 1 << e
    return m


def halves(seq):
    h = len(seq) // 2
    return [seq[:h], seq[h:]]


def layout(T, topo):
    cores = [int(c) for c in T.cores]
    L = []
    for j, c in enumerate(cores):
        near = [r for r in range(N) if topo.chip(cores[r]) == topo.chip(c)]
        far = [r for r in range(N) if topo.chip(cores[r]) != topo.chip(c)]
        L.append({"core": c, "near": near, "far": far,
                  "direct": all(topo.may_write(c, cores[r]) for r in far)})
    for j, e in enumerate(L):
        c = e["core"]
        like = [r for r in e["near"] if L[r]["direct"] == e["direct"]]
        p = like.index(j) % 2
        fh = halves(e["far"])
        e["first"], e["second"] = fh[p], fh[1 - p]
        nh = halves(e["near"])
        k = e["near"].index(j) // 2
        e["own_pair"], e["other_pair"] = nh[k], nh[1 - k]
        e["partner"] = [r for r in nh[k] if r != j][0]
        e["slot"] = {r: r for r in range(N)}
        e["relays"] = []
        if not e["direct"]:
            fchip = topo.chip(cores[e["far"][0]])
            e["relays"] = [h for h in range(SIM_CORES)
                           if T.rank_of(h) is None and topo.mates(topo.chip(h), fchip)
                           and topo.same_plane(topo.chip(h), topo.chip(c)) and topo.die(h) == topo.die(c)
                           and topo.may_write(c, h) and all(topo.may_write(h, cores[r]) for r in e["far"])][:2]
            a, b, base = e["first"], e["second"], e["far"][0]
            for i, r in enumerate((a[0], b[0], a[1], b[1])):
                e["slot"][r] = base + i
    return L


def calls_of(L, topo, c):
    cores = [e["core"] for e in L]
    out = []
    for j, e in enumerate(L):
        arr = "arr%d" % j
        a, b, slot = e["first"], e["second"], e["slot"]
        if e["core"] == c:
            off = bits(topo.mask(c, cores[e["far"][0]] if e["direct"] else e["relays"][0]))
            hi = [x for x in bits(topo.mask(c, cores[e["partner"]])) if x not in off]
            if e["direct"]:
                for pair in (a, b):
                    for kind in "qs":
                        out.append((["qd%d" % r for r in pair] if kind == "q" else [],
                                    [(kind, "x", slot[r], 1, cores[r], j, halves(off)[i], arr)
                                     for i, r in enumerate(pair)]))
            else:
                for i, r in enumerate((a[0], a[1], b[0], b[1])):
                    out.append((["qd%d" % r],
                                [("q", "x", slot[r], 1, e["relays"][i % 2], slot[r], off, "h%d" % (i // 2))]))
                out.append(([], [("s", "x", slot[a[k]], 2, e["relays"][k], slot[a[k]], halves(off)[k], "h2")
                                 for k in range(2)]))
            for kind in "qs":
                out.append((["qd%d" % r for r in e["other_pair"]] if kind == "q" else [],
                            [(kind, "x", slot[r], 1, cores[r], j, halves(hi)[i], arr)
                             for i, r in enumerate(e["other_pair"])]))
            r = e["partner"]
            for kind in "qs":
                out.append((["qd%d" % r] if kind == "q" else [], [(kind, "x", slot[r], 1, cores[r], j, hi, arr)]))
        for k, h in enumerate(e["relays"]):
            if h == c:
                for i, r in enumerate((a[k], b[k])):
                    out.append((["h%d" % i], [("q", "r", slot[r], 1, cores[r], j, bits(topo.mask(c, cores[r])), arr)]))
                out.append((["h2"], [("s", "r", slot[r], 1, cores[r], j, halves(bits(topo.mask(c, cores[r])))[i], arr)
                                     for i, r in enumerate((a[k], b[k]))]))
    return out


def view(T, kind, where, slot, n):
    lo, hi = NC * slot, NC * (slot + n)
    if kind == "q":
        return (T.qx if where == "x" else T.rq)[:, lo:hi].bitcast(dt.uint8)
    return (T.sx if where == "x" else T.rs)[:, lo:hi]


def rank_program(g, core, T, topo):
    L = layout(T, topo)
    busy = [e["core"] for e in L] + [h for e in L for h in e["relays"]]
    if core not in busy:
        return
    total = {}
    for c in busy:
        for waits, trs in calls_of(L, topo, c):
            for t in trs:
                total[(t[4], t[7])] = total.get((t[4], t[7]), 0) + len(t[6])

    rank = T.rank_of(core)
    if rank is not None:
        e = L[rank]
        loads = [(e["first"], g.sync), (e["second"], g.scalar), (e["other_pair"], g.sync), (e["own_pair"], g.scalar)]
        for i, (pair, q) in enumerate(loads):
            lo, hi = XC * pair[0], XC * (pair[1] + 1)
            q.dma_start(T.xb[:, lo:hi], T.x[:, lo:hi]).then_inc(T.sem["ld%d" % i], 16)
        g.sync.dma_start(T.wb[:], T.w[:]).then_inc(T.sem.ld4, 16)
        for i, (pair, q) in enumerate(loads):
            g.vector.wait_ge(T.sem["ld%d" % i], 16)
            for r in sorted(pair, key=lambda t: t == rank):
                qb, sb, s = (T.rq, T.rs, rank) if r == rank else (T.qx, T.sx, e["slot"][r])
                g.vector.quantize_mx(qb[:, NC * s:NC * (s + 1)], sb[:, NC * s:NC * (s + 1)],
                                     T.xb[:, XC * r:XC * (r + 1)]).then_inc(T.sem["qd%d" % r], 1)
        g.vector.wait_ge(T.sem.ld4, 16)
        g.vector.quantize_mx(T.qw[:], T.sw[:], T.wb[:]).then_inc(T.sem.qdw, 1)

    sent = 0
    for waits, trs in calls_of(L, topo, core):
        for s in waits:
            g.wait_ge(T.sem[s], total.get((core, s), 1))
        if len(trs) == 1:
            kind, where, slot, n, dst, dslot, engines, sem = trs[0]
            rid, pid, ring = topo.addr(dst)
            g.remote_dma(out_ap=view(T, kind, "r", dslot, n), in_ap=view(T, kind, where, slot, n),
                         remote_sem=T.sem[sem], local_sem=T.sem.sent, pid=pid, routing_id=rid,
                         dma_engine_mask=to_mask(engines))
        else:
            batch = []
            for kind, where, slot, n, dst, dslot, engines, sem in trs:
                rid, pid, ring = topo.addr(dst)
                batch.append(RemoteDMATransfer(dst_ids=[DstId(rid=rid, pnc=pid)], dma_engine_mask=to_mask(engines),
                                               remote_sem=T.sem[sem], src=view(T, kind, where, slot, n),
                                               dst=view(T, kind, "r", dslot, n)))
            g.remote_dma_fused(batch, local_sem=T.sem.sent)
        sent += sum(len(t[6]) for t in trs)
    g.wait_ge(T.sem.sent, sent)
    if rank is None:
        return

    def arr(s):
        return "arr%d" % s
    fd = [s for s in e["far"] if L[s]["direct"]]
    units = [(e["other_pair"][0], 2, [arr(s) for s in e["other_pair"]])]
    units += [(s, 1, [arr(s)]) for s in fd if rank in L[s]["first"]]
    units += [(e["own_pair"][0], 2, ["qd%d" % rank, arr(e["partner"])])]
    units += [(s, 1, [arr(s)]) for s in fd if rank not in L[s]["first"]]
    units += [(s, 1, [arr(s)]) for s in e["far"] if not L[s]["direct"]]
    g.tensor.wait_ge(T.sem.qdw, 1)
    stores = {"stA": 0, "stB": 0}
    for u, (blk, n, sems) in enumerate(units):
        lo, hi = NC * blk, NC * (blk + n)
        bank = T.ps[:, 512 * u:512 * u + NC * n]
        for s in sems:
            g.tensor.wait_ge(T.sem[s], total.get((core, s), 1))
        g.tensor.matmul_mx(bank, T.qw[:], T.sw[:], T.rq[:, lo:hi], T.rs[:, lo:hi], True, True).then_inc(T.sem["mm%d" % u], 1)
        if u % 2 == 0:
            g.vector.wait_ge(T.sem["mm%d" % u], 1)
            g.vector.tensor_copy(T.yb[:, lo:hi], bank).then_inc(T.sem["cp%d" % u], 1)
            q, st = g.sync, "stA"
        else:
            g.scalar.wait_ge(T.sem["mm%d" % u], 1)
            g.scalar.activation(T.yb[:, lo:hi], bank, ActivationFunctionType.Copy).then_inc(T.sem["cp%d" % u], 1)
            q, st = g.scalar, "stB"
        q.wait_ge(T.sem["cp%d" % u], 1)
        q.dma_start(T.y[:, lo:hi], T.yb[:, lo:hi]).then_inc(T.sem[st], 16)
        stores[st] += 16
    g.sync.wait_ge(T.sem.stA, stores["stA"])
    g.scalar.wait_ge(T.sem.stB, stores["stB"])
